import numpy as np
import ml_dtypes


def mxq(x, axis, fmt="e4m3"):
    dtype, down = {"e4m3": (ml_dtypes.float8_e4m3fn, 7), "e5m2": (ml_dtypes.float8_e5m2, 14)}[fmt]
    v = np.moveaxis(np.asarray(x, np.float32).astype(ml_dtypes.bfloat16).astype(np.float64), axis, -1)
    blocks = v.reshape(v.shape[:-1] + (-1, 32))
    amax = np.abs(blocks).max(-1, keepdims=True)
    byte = np.maximum(np.where(amax > 0, np.frexp(amax)[1] - 1 + 127, 0) - down, 1)
    scale = np.exp2(byte - 127.0)
    codes = (blocks / scale).astype(np.float32).astype(dtype).astype(np.float64)
    return np.moveaxis((codes * scale).reshape(v.shape), -1, axis)


WIDE = False


def mx_kscale(k):
    if not WIDE:
        return np.ones(k)
    levels = np.array([10, -10, 5, -5, 0])
    if k % 512:
        return np.exp2(np.random.permutation(np.resize(levels, k // 32))).repeat(32)
    a = np.empty((k // 512, 16))
    for p in range(k // 512):
        a[p, :8] = np.random.permutation(np.resize(levels, 8))
        for g in range(8):
            far = levels[np.abs(levels - a[p, g]) >= 10]
            a[p, g + 8] = far[np.random.randint(len(far))]
    return np.exp2(a.ravel()).repeat(32)


def f64(x):
    return np.asarray(x).astype(np.float64)


def striped(idx):
    return np.tile(np.asarray(idx).reshape(-1, 16).T, (8, 1)).astype(np.uint16)


def unstriped(offs):
    return offs[:16].T.reshape(-1).astype(np.int64)


E2M1 = np.array([0.0, 0.5, 1.0, 1.5, 2.0, 3.0, 4.0, 6.0, -0.0, -0.5, -1.0, -1.5, -2.0, -3.0, -4.0, -6.0])


def pack_weight(w, fmt):
    k, n = w.shape
    w = f64(np.asarray(w, np.float32).astype(ml_dtypes.bfloat16)).reshape(k // 32, 32, n)
    amax = np.abs(w).max(1)
    if fmt == "e4m3":
        byte = np.frexp(amax)[1] - 1 + 127 - 7
    else:
        mant, ex = np.frexp(amax / 6.0)
        byte = np.where(mant > 0.5, ex, ex - 1) + 127
    byte = np.clip(np.where(amax > 0, byte, 1), 1, 254)
    scaled = (w * np.exp2(127.0 - byte)[:, None, :]).reshape(k, n).astype(np.float32)
    by_word = np.ascontiguousarray(scaled.reshape(k // 512, 128, 4, n).transpose(0, 1, 3, 2))
    if fmt == "e4m3":
        words = by_word.astype(ml_dtypes.float8_e4m3fn).view(np.uint8)
    else:
        c = by_word.astype(ml_dtypes.float4_e2m1fn).view(np.uint8) & 0xF
        words = (c[..., 0::2] | (c[..., 1::2] << 4)).reshape(k // 512, 128, 2 * n)
    return np.ascontiguousarray(words), np.ascontiguousarray(byte.astype(np.uint8).reshape(k // 512, 16, n))


def unpack_weight(words, scales, fmt):
    g, _, n = scales.shape
    words = np.ascontiguousarray(words).reshape(g, 128, n, -1)
    if fmt == "e4m3":
        vals = words.view(ml_dtypes.float8_e4m3fn).astype(np.float64)
    else:
        nib = np.empty((g, 128, n, 4), np.uint8)
        nib[..., 0::2] = words & 0xF
        nib[..., 1::2] = words >> 4
        vals = E2M1[nib]
    vals = vals * np.repeat(np.exp2(scales.astype(np.float64) - 127.0), 8, axis=1)[..., None]
    return vals.transpose(0, 1, 3, 2).reshape(g * 512, n)


D, T, I, Q, K, M = 512, 2048, 512, 128, 16, 2048


def setup_inputs():
    n = np.random.standard_normal
    idx = np.random.permutation(T)[:I]
    idx2 = np.random.permutation(M)[:I]
    fd = mx_kscale(D)
    keysp = pack_weight(n((D, T)) / fd[:, None], "e4m3")
    return {
        "query": (n((D, Q)) * 1.0 / np.sqrt(D) * fd[:, None]).astype(np.float32),
        "keys_words": keysp[0],
        "keys_scales": keysp[1],
        "lowend": np.tile(np.random.uniform(-1.5, 0.0, T), (128, 1)).astype(np.float32),
        "highend": np.tile(np.random.uniform(0.0, 1.5, T), (128, 1)).astype(np.float32),
        "lam": (np.random.uniform(0.8, 2.0, (Q, 1))).astype(np.float32),
        "old": (np.random.uniform(0.0, 2.0, (Q, M))).astype(np.float32),
        "fade": (np.random.uniform(0.3, 0.9, (Q, 1))).astype(np.float32),
        "offs": striped(idx),
        "offs2": striped(idx2),
    }


def reference(query, keys_words, keys_scales, lowend, highend, lam, old, fade, offs, offs2):
    idx = unstriped(offs)
    idx2 = unstriped(offs2)
    keysu = unpack_weight(keys_words, keys_scales, "e4m3")
    queryq = mxq(f64(query), 0, "e4m3")
    keysidxg = keysu[:, idx]
    a = queryq.T @ keysidxg
    s = np.minimum(a - f64(lowend)[:1][:, idx], f64(highend)[:1][:, idx] - a) * f64(lam)
    p = np.exp(s - np.max(s, axis=1, keepdims=True))
    r = p / np.sum(p, axis=1, keepdims=True)
    rt = r.T
    rg = rt.reshape(I, K, Q // K).sum(axis=2)
    rq = 1.0 / np.sqrt(rg)
    rr = np.repeat(rq, Q // K, axis=1)
    w0 = rt * rr
    w = w0.T
    ws = w * 128.0
    wf = np.zeros((Q, M))
    wf[:, idx2] = ws
    y = f64(old) * f64(fade) + wf
    return y

@@ -1,0 +1,191 @@
+from contextlib import ExitStack
+
+import concourse.mybir as mybir
+from concourse.masks import make_identity
+
+D, T, I, Q, K, M = 512, 2048, 512, 128, 16, 2048
+FLOPS = 2 * D * Q * I
+BYTES = 4 * D * Q + D * T + (D // 32) * T + 2 * 4 * T + 2 * 4 * Q + 2 * 4 * Q * M + 2 * 2 * 128 * (I // 16)
+
+F32 = mybir.dt.float32
+BF16 = mybir.dt.bfloat16
+I32 = mybir.dt.int32
+U32 = mybir.dt.uint32
+U16 = mybir.dt.uint16
+U8 = mybir.dt.uint8
+FP8X4 = mybir.dt.float8_e4m3fn_x4
+ALU = mybir.AluOpType
+ACT = mybir.ActivationFunctionType
+
+P = 128
+PACK = 4
+GROUP = Q // K
+CHUNK = 128
+CHUNKS = I // CHUNK
+HALF = I // 2
+LIVE = P - 1
+STORE_WIDTHS = (256, 512, 512, 512, 256)
+
+
+def tile_attend_interval_balanced_counts_kernel(
+    tc, query, keys_words, keys_scales, lowend, highend, lam, old, fade, offs, offs2, out
+):
+    nc = tc.nc
+    with ExitStack() as ctx:
+        sb = ctx.enter_context(tc.tile_pool(name="sb", bufs=1))
+        ps = ctx.enter_context(tc.psum_pool(name="ps", bufs=1))
+
+        gather_list = sb.tile([P, I // 16], U16, name="gather_list")
+        scatter_list = sb.tile([P, I // 16], U16, name="scatter_list")
+        key_words = sb.tile([P, T], U32, name="key_words")
+        key_scales = sb.tile([P, T], U8, name="key_scales")
+        low_pool = sb.tile([P, T], F32, name="low_pool")
+        high_pool = sb.tile([P, T], F32, name="high_pool", tag="high_pool_then_low_cols")
+        q_raw = sb.tile([P, PACK, Q], F32, name="q_raw", tag="q_raw_then_old")
+        lam_col = sb.tile([P, 1], F32, name="lam_col")
+        fade_col = sb.tile([P, 1], F32, name="fade_col")
+
+        scale_words = key_scales[:].bitcast(I32)
+        nc.gpsimd.memset(scale_words, 0)
+        one = sb.tile([P, 1], F32, name="one")
+        nc.gpsimd.memset(one[:], 1.0)
+        tiny = sb.tile([P, 1], F32, name="tiny")
+        nc.scalar.activation(tiny[:], one[:], ACT.Copy, scale=1e-30)
+        nc.sync.dma_start(gather_list[:], offs)
+        for r in range(4):
+            nc.sync.dma_start(scale_words[r:P:32, :], keys_scales[0, r::4, :].bitcast(I32))
+        nc.sync.dma_start(low_pool[LIVE:P, :], lowend[0:1, :])
+        nc.sync.dma_start(high_pool[LIVE:P, :], highend[0:1, :])
+        nc.sync.dma_start(key_words[:].bitcast(I32), keys_words[0].rearrange("p n t -> p (n t)").bitcast(I32))
+        nc.sync.dma_start(q_raw[:], query.rearrange("(p j) q -> p j q", j=PACK))
+        nc.sync.dma_start(scatter_list[:], offs2)
+        nc.vector.memset(low_pool[0:LIVE, :], 0.0)
+        nc.vector.memset(high_pool[0:LIVE, :], 0.0)
+
+        ident = sb.tile([P, P], F32, name="ident")
+        make_identity(nc, ident[:])
+        nc.gpsimd.dma_start(lam_col[:], lam)
+        nc.gpsimd.dma_start(fade_col[:], fade)
+
+        turned = []
+        for name, pool_tile in (("low", low_pool), ("high", high_pool)):
+            picked = sb.tile([P, I], F32, name=name + "_picked")
+            nc.scalar.activation(picked[:], pool_tile[:].indirect(gather_list[:]), ACT.Copy)
+            bank = ps.tile([P, CHUNKS, P], F32, name=name + "_turned", tag=name + "_bank")
+            for c in range(CHUNKS):
+                nc.tensor.transpose(bank[:, c, :], picked[:, c * CHUNK : (c + 1) * CHUNK], ident[:])
+            turned.append(bank)
+        low_cols = sb.tile([P, CHUNKS], F32, name="low_cols", tag="high_pool_then_low_cols")
+        nc.scalar.copy(low_cols[:], turned[0][:, :, LIVE])
+
+        q_grouped = sb.tile([P, Q, PACK], BF16, name="q_grouped", align_bytes=64)
+        nc.scalar.copy(out=q_grouped[:], in_=q_raw[:].rearrange("p j q -> p q j"))
+        q_codes = sb.tile([P, Q], U32, name="q_codes", tag="q_codes_then_window", align_bytes=64)
+        q_scales = sb.tile([P, Q], U8, name="q_scales", align_bytes=64)
+        nc.vector.quantize_mx(
+            out=q_codes[:].bitcast(FP8X4), scales=q_scales[:], in_=q_grouped[:].rearrange("p q j -> p (q j)")
+        )
+
+        high_cols = sb.tile([P, CHUNKS], F32, name="high_cols", tag="q_raw_then_old")
+        nc.scalar.copy(high_cols[:], turned[1][:, :, LIVE])
+
+        picked_scales = sb.tile([P, I], U8, name="picked_scales", align_bytes=64)
+        nc.vector.tensor_copy(picked_scales[:], key_scales[:].indirect(gather_list[:]))
+
+        products = []
+        for c in range(CHUNKS):
+            picked_words = sb.tile([P, CHUNK], U32, name="picked_words%d" % c, align_bytes=64)
+            nc.vector.tensor_copy(picked_words[:], key_words[:].indirect(gather_list[:, 8 * c : 8 * (c + 1)]))
+            product = ps.tile([P, Q], F32, name="product%d" % c, tag=("low_bank", "high_bank", "bank2", "bank3")[c])
+            nc.tensor.matmul_mx(
+                out=product[:],
+                lhsT=picked_words[:].bitcast(FP8X4),
+                lhsT_scale=picked_scales[:, c * CHUNK : (c + 1) * CHUNK],
+                rhs=q_codes[:].bitcast(FP8X4),
+                rhs_scale=q_scales[:],
+                start=True,
+                stop=True,
+            )
+            products.append(product)
+
+        window = sb.tile([P, M], F32, name="window", tag="q_codes_then_window", align_bytes=64)
+        nc.gpsimd.memset(window[:], 0.0)
+
+        neg_margin_t = [ps.tile([P, 2, P], F32, name="neg_margin_t%d" % h) for h in range(2)]
+        for c in range(CHUNKS):
+            below = sb.tile([P, Q], F32, name="below%d" % c)
+            nc.scalar.activation(below[:], products[c][:], ACT.Identity, bias=low_cols[:, c : c + 1], scale=-1.0)
+            neg_margin = sb.tile([P, Q], F32, name="neg_margin%d" % c)
+            nc.vector.scalar_tensor_tensor(
+                neg_margin[:], products[c][:], high_cols[:, c : c + 1], below[:], ALU.subtract, ALU.max
+            )
+            nc.tensor.transpose(neg_margin_t[c // 2][:, c % 2, :], neg_margin[:], ident[:])
+
+        old_sb = sb.tile([P, M], F32, name="old_sb", tag="q_raw_then_old")
+        nc.sync.dma_start(old_sb[:], old)
+
+        neg_score = sb.tile([P, I], F32, name="neg_score")
+        neg_max = [sb.tile([P, 1], F32, name="neg_max%d" % h) for h in range(2)]
+        for h in range(2):
+            nc.vector.tensor_scalar(
+                neg_score[:, h * HALF : (h + 1) * HALF],
+                neg_margin_t[h][:].rearrange("p c s -> p (c s)"),
+                lam_col[:],
+                neg_max[0][:] if h else None,
+                ALU.mult,
+                ALU.min,
+                accum_out=neg_max[h][:],
+            )
+
+        p_exp = sb.tile([P, I], F32, name="p_exp")
+        row_sum = sb.tile([P, 1], F32, name="row_sum")
+        nc.scalar.activation(p_exp[:], neg_score[:], ACT.Exp, bias=neg_max[1][:], scale=-1.0, accum_out=row_sum[:])
+        row_inv = sb.tile([P, 1], F32, name="row_inv")
+        nc.vector.reciprocal(row_inv[:], row_sum[:])
+
+        shares = [sb.tile([P, HALF], F32, name="share%d" % h) for h in range(2)]
+        share_t = []
+        for h in range(2):
+            nc.vector.tensor_scalar(shares[h][:], p_exp[:, h * HALF : (h + 1) * HALF], row_inv[:], None, ALU.mult)
+            bank = ps.tile([P, 2, P], F32, name="share_t%d" % h, tag="share_bank%d" % h)
+            for c in range(2):
+                nc.tensor.transpose(bank[:, c, :], shares[h][:, c * CHUNK : (c + 1) * CHUNK], ident[:])
+            share_t.append(bank)
+
+        factors = []
+        for h in range(2):
+            group_sum = sb.tile([P, 2 * K], F32, name="group_sum%d" % h)
+            nc.vector.tensor_reduce(
+                group_sum[:],
+                share_t[h][:].rearrange("p c (k j) -> p (c k) j", j=GROUP),
+                mybir.AxisListType.X,
+                ALU.add,
+            )
+            factor_t = sb.tile([P, 2 * K, GROUP], F32, name="factor_t%d" % h)
+            nc.scalar.activation(
+                factor_t[:],
+                group_sum[:].unsqueeze(2).to_broadcast([P, 2 * K, GROUP]),
+                ACT.Abs_reciprocal_sqrt,
+                bias=tiny[:],
+                scale=1.0 / (128.0 * 128.0),
+            )
+            bank = ps.tile([P, 2, P], F32, name="factor_bank%d" % h, tag=("low_bank", "high_bank")[h])
+            flat = factor_t[:].rearrange("p g j -> p (g j)")
+            for c in range(2):
+                nc.tensor.transpose(bank[:, c, :], flat[:, c * Q : (c + 1) * Q], ident[:])
+            factors.append(bank)
+
+        for h in range(2):
+            factor = sb.tile([P, HALF], F32, name="factor%d" % h)
+            nc.scalar.copy(factor[:], factors[h][:].rearrange("p c s -> p (c s)"))
+            nc.vector.tensor_tensor(
+                window[:].indirect(scatter_list[:, 16 * h : 16 * (h + 1)]), shares[h][:], factor[:], ALU.mult
+            )
+
+        start = 0
+        for n, width in enumerate(STORE_WIDTHS):
+            cols = slice(start, start + width)
+            result = sb.tile([P, width], F32, name="result%d" % n)
+            nc.vector.scalar_tensor_tensor(result[:], old_sb[:, cols], fade_col[:], window[:, cols], ALU.mult, ALU.add)
+            (nc.sync, nc.scalar)[n % 2].dma_start(out[:, cols], result[:])
+            start += width

@@ -24,7 +24,8 @@ CHUNK = 128
 CHUNKS = I // CHUNK
 HALF = I // 2
 LIVE = P - 1
-STORE_WIDTHS = (256, 512, 512, 512, 256)
+HIGH_SPLIT = 512
+STORE_WIDTHS = (512, 512, 512, 512)
 
 
 def tile_attend_interval_balanced_counts_kernel(
@@ -39,7 +40,7 @@ def tile_attend_interval_balanced_counts_kernel(
         scatter_list = sb.tile([P, I // 16], U16, name="scatter_list")
         key_words = sb.tile([P, T], U32, name="key_words")
         key_scales = sb.tile([P, T], U8, name="key_scales")
-        low_pool = sb.tile([P, T], F32, name="low_pool")
+        low_pool = sb.tile([P, T], F32, name="low_pool", tag="low_pool_then_words", align_bytes=64)
         high_pool = sb.tile([P, T], F32, name="high_pool", tag="high_pool_then_low_cols")
         q_raw = sb.tile([P, PACK, Q], F32, name="q_raw", tag="q_raw_then_old")
         lam_col = sb.tile([P, 1], F32, name="lam_col")
@@ -49,58 +50,63 @@ def tile_attend_interval_balanced_counts_kernel(
         nc.gpsimd.memset(scale_words, 0)
         one = sb.tile([P, 1], F32, name="one")
         nc.gpsimd.memset(one[:], 1.0)
-        tiny = sb.tile([P, 1], F32, name="tiny")
-        nc.scalar.activation(tiny[:], one[:], ACT.Copy, scale=1e-30)
         nc.sync.dma_start(gather_list[:], offs)
-        for r in range(4):
-            nc.sync.dma_start(scale_words[r:P:32, :], keys_scales[0, r::4, :].bitcast(I32))
         nc.sync.dma_start(low_pool[LIVE:P, :], lowend[0:1, :])
         nc.sync.dma_start(high_pool[LIVE:P, :], highend[0:1, :])
-        nc.sync.dma_start(key_words[:].bitcast(I32), keys_words[0].rearrange("p n t -> p (n t)").bitcast(I32))
+        for r in range(4):
+            queue = nc.gpsimd if r == 3 else nc.sync
+            queue.dma_start(scale_words[32 * r : 32 * r + 4, :], keys_scales[0, 4 * r : 4 * r + 4, :].bitcast(I32))
         nc.sync.dma_start(q_raw[:], query.rearrange("(p j) q -> p j q", j=PACK))
+        nc.sync.dma_start(key_words[:].bitcast(I32), keys_words[0].rearrange("p n t -> p (n t)").bitcast(I32))
+        tiny = sb.tile([P, 1], F32, name="tiny")
+        nc.scalar.activation(tiny[:], one[:], ACT.Copy, scale=1e-30)
+        nc.sync.dma_start(lam_col[:], lam)
         nc.sync.dma_start(scatter_list[:], offs2)
-        nc.vector.memset(low_pool[0:LIVE, :], 0.0)
-        nc.vector.memset(high_pool[0:LIVE, :], 0.0)
-
+        nc.sync.dma_start(fade_col[:], fade)
+        nc.vector.memset(low_pool[0:LIVE, 0 : T // 2 - 1], 0.0)
+        nc.vector.memset(low_pool[0:LIVE, T // 2 - 1 : T], 0.0)
+        nc.vector.memset(high_pool[0:LIVE, 0 : HIGH_SPLIT // 2 - 1], 0.0)
+        nc.vector.memset(high_pool[0:LIVE, HIGH_SPLIT // 2 - 1 : HIGH_SPLIT], 0.0)
         ident = sb.tile([P, P], F32, name="ident")
         make_identity(nc, ident[:])
-        nc.gpsimd.dma_start(lam_col[:], lam)
-        nc.gpsimd.dma_start(fade_col[:], fade)
+        nc.gpsimd.memset(high_pool[0:LIVE, HIGH_SPLIT:T], 0.0)
 
+        q_grouped = sb.tile([P, Q, PACK], BF16, name="q_grouped", align_bytes=64)
+        nc.scalar.copy(out=q_grouped[:], in_=q_raw[:].rearrange("p j q -> p q j"))
+        q_codes = sb.tile([P, Q], U32, name="q_codes", tag="q_codes_then_window", align_bytes=64)
+        q_scales = sb.tile([P, Q], U8, name="q_scales", align_bytes=64)
+
+        low_picked = sb.tile([P, I], F32, name="low_picked")
+        nc.vector.tensor_copy(low_picked[:], low_pool[:].indirect(gather_list[:]))
+        high_picked = sb.tile([P, I], F32, name="high_picked")
+        nc.scalar.activation(high_picked[:], high_pool[:].indirect(gather_list[:]), ACT.Copy)
+        nc.vector.quantize_mx(
+            out=q_codes[:].bitcast(FP8X4), scales=q_scales[:], in_=q_grouped[:].rearrange("p q j -> p (q j)")
+        )
         turned = []
-        for name, pool_tile in (("low", low_pool), ("high", high_pool)):
-            picked = sb.tile([P, I], F32, name=name + "_picked")
-            nc.scalar.activation(picked[:], pool_tile[:].indirect(gather_list[:]), ACT.Copy)
+        for name, picked in (("low", low_picked), ("high", high_picked)):
             bank = ps.tile([P, CHUNKS, P], F32, name=name + "_turned", tag=name + "_bank")
             for c in range(CHUNKS):
                 nc.tensor.transpose(bank[:, c, :], picked[:, c * CHUNK : (c + 1) * CHUNK], ident[:])
             turned.append(bank)
         low_cols = sb.tile([P, CHUNKS], F32, name="low_cols", tag="high_pool_then_low_cols")
         nc.scalar.copy(low_cols[:], turned[0][:, :, LIVE])
-
-        q_grouped = sb.tile([P, Q, PACK], BF16, name="q_grouped", align_bytes=64)
-        nc.scalar.copy(out=q_grouped[:], in_=q_raw[:].rearrange("p j q -> p q j"))
-        q_codes = sb.tile([P, Q], U32, name="q_codes", tag="q_codes_then_window", align_bytes=64)
-        q_scales = sb.tile([P, Q], U8, name="q_scales", align_bytes=64)
-        nc.vector.quantize_mx(
-            out=q_codes[:].bitcast(FP8X4), scales=q_scales[:], in_=q_grouped[:].rearrange("p q j -> p (q j)")
-        )
-
         high_cols = sb.tile([P, CHUNKS], F32, name="high_cols", tag="q_raw_then_old")
         nc.scalar.copy(high_cols[:], turned[1][:, :, LIVE])
 
         picked_scales = sb.tile([P, I], U8, name="picked_scales", align_bytes=64)
         nc.vector.tensor_copy(picked_scales[:], key_scales[:].indirect(gather_list[:]))
 
+        picked_words = sb.tile([P, I], U32, name="picked_words", tag="low_pool_then_words", align_bytes=64)
         products = []
         for c in range(CHUNKS):
-            picked_words = sb.tile([P, CHUNK], U32, name="picked_words%d" % c, align_bytes=64)
-            nc.vector.tensor_copy(picked_words[:], key_words[:].indirect(gather_list[:, 8 * c : 8 * (c + 1)]))
+            slots = slice(c * CHUNK, (c + 1) * CHUNK)
+            nc.vector.tensor_copy(picked_words[:, slots], key_words[:].indirect(gather_list[:, 8 * c : 8 * (c + 1)]))
             product = ps.tile([P, Q], F32, name="product%d" % c, tag=("low_bank", "high_bank", "bank2", "bank3")[c])
             nc.tensor.matmul_mx(
                 out=product[:],
-                lhsT=picked_words[:].bitcast(FP8X4),
-                lhsT_scale=picked_scales[:, c * CHUNK : (c + 1) * CHUNK],
+                lhsT=picked_words[:, slots].bitcast(FP8X4),
+                lhsT_scale=picked_scales[:, slots],
                 rhs=q_codes[:].bitcast(FP8X4),
                 rhs_scale=q_scales[:],
                 start=True,
@@ -111,7 +117,9 @@ def tile_attend_interval_balanced_counts_kernel(
         window = sb.tile([P, M], F32, name="window", tag="q_codes_then_window", align_bytes=64)
         nc.gpsimd.memset(window[:], 0.0)
 
-        neg_margin_t = [ps.tile([P, 2, P], F32, name="neg_margin_t%d" % h) for h in range(2)]
+        early = (CHUNKS - 1) * CHUNK
+        spans = (slice(0, early), slice(early, I))
+        neg_margin_t = [ps.tile([P, I], F32, name="neg_margin_t%d" % h) for h in range(2)]
         for c in range(CHUNKS):
             below = sb.tile([P, Q], F32, name="below%d" % c)
             nc.scalar.activation(below[:], products[c][:], ACT.Identity, bias=low_cols[:, c : c + 1], scale=-1.0)
@@ -119,7 +127,8 @@ def tile_attend_interval_balanced_counts_kernel(
             nc.vector.scalar_tensor_tensor(
                 neg_margin[:], products[c][:], high_cols[:, c : c + 1], below[:], ALU.subtract, ALU.max
             )
-            nc.tensor.transpose(neg_margin_t[c // 2][:, c % 2, :], neg_margin[:], ident[:])
+            bank = neg_margin_t[c // (CHUNKS - 1)]
+            nc.tensor.transpose(bank[:, c * CHUNK : (c + 1) * CHUNK], neg_margin[:], ident[:])
 
         old_sb = sb.tile([P, M], F32, name="old_sb", tag="q_raw_then_old")
         nc.sync.dma_start(old_sb[:], old)
@@ -128,8 +137,8 @@ def tile_attend_interval_balanced_counts_kernel(
         neg_max = [sb.tile([P, 1], F32, name="neg_max%d" % h) for h in range(2)]
         for h in range(2):
             nc.vector.tensor_scalar(
-                neg_score[:, h * HALF : (h + 1) * HALF],
-                neg_margin_t[h][:].rearrange("p c s -> p (c s)"),
+                neg_score[:, spans[h]],
+                neg_margin_t[h][:, spans[h]],
                 lam_col[:],
                 neg_max[0][:] if h else None,
                 ALU.mult,
@@ -143,43 +152,43 @@ def tile_attend_interval_balanced_counts_kernel(
         row_inv = sb.tile([P, 1], F32, name="row_inv")
         nc.vector.reciprocal(row_inv[:], row_sum[:])
 
-        shares = [sb.tile([P, HALF], F32, name="share%d" % h) for h in range(2)]
-        share_t = []
+        shares = [sb.tile([P, HALF], F32, name="share%d" % h, align_bytes=64) for h in range(2)]
         for h in range(2):
             nc.vector.tensor_scalar(shares[h][:], p_exp[:, h * HALF : (h + 1) * HALF], row_inv[:], None, ALU.mult)
-            bank = ps.tile([P, 2, P], F32, name="share_t%d" % h, tag="share_bank%d" % h)
-            for c in range(2):
-                nc.tensor.transpose(bank[:, c, :], shares[h][:, c * CHUNK : (c + 1) * CHUNK], ident[:])
-            share_t.append(bank)
+        share_blocks = sb.tile([P, HALF], F32, name="share_blocks", align_bytes=64)
+        nc.vector.transpose(share_blocks[:], shares[0][:])
+        share_bank = ps.tile([P, HALF], F32, name="share_bank")
+        for c in range(2):
+            cols = slice(c * CHUNK, (c + 1) * CHUNK)
+            nc.tensor.transpose(share_bank[:, cols], shares[1][:, cols], ident[:])
 
-        factors = []
-        for h in range(2):
-            group_sum = sb.tile([P, 2 * K], F32, name="group_sum%d" % h)
+        turned_factors = []
+        for h, turned_share in enumerate((share_blocks, share_bank)):
+            group_sum = sb.tile([P, HALF // GROUP], F32, name="group_sum%d" % h)
             nc.vector.tensor_reduce(
-                group_sum[:],
-                share_t[h][:].rearrange("p c (k j) -> p (c k) j", j=GROUP),
-                mybir.AxisListType.X,
-                ALU.add,
+                group_sum[:], turned_share[:].rearrange("p (g j) -> p g j", j=GROUP), mybir.AxisListType.X, ALU.add
             )
-            factor_t = sb.tile([P, 2 * K, GROUP], F32, name="factor_t%d" % h)
+            turned_factor = sb.tile([P, HALF], F32, name="turned_factor%d" % h, align_bytes=64)
             nc.scalar.activation(
-                factor_t[:],
-                group_sum[:].unsqueeze(2).to_broadcast([P, 2 * K, GROUP]),
+                turned_factor[:].rearrange("p (g j) -> p g j", j=GROUP),
+                group_sum[:].unsqueeze(2).to_broadcast([P, HALF // GROUP, GROUP]),
                 ACT.Abs_reciprocal_sqrt,
                 bias=tiny[:],
                 scale=1.0 / (128.0 * 128.0),
             )
-            bank = ps.tile([P, 2, P], F32, name="factor_bank%d" % h, tag=("low_bank", "high_bank")[h])
-            flat = factor_t[:].rearrange("p g j -> p (g j)")
-            for c in range(2):
-                nc.tensor.transpose(bank[:, c, :], flat[:, c * Q : (c + 1) * Q], ident[:])
-            factors.append(bank)
+            turned_factors.append(turned_factor)
+
+        factors = [sb.tile([P, HALF], F32, name="factor%d" % h, align_bytes=64) for h in range(2)]
+        nc.vector.transpose(factors[0][:], turned_factors[0][:])
+        factor_bank = ps.tile([P, HALF], F32, name="factor_bank")
+        for c in range(2):
+            cols = slice(c * CHUNK, (c + 1) * CHUNK)
+            nc.tensor.transpose(factor_bank[:, cols], turned_factors[1][:, cols], ident[:])
+        nc.scalar.copy(factors[1][:], factor_bank[:])
 
         for h in range(2):
-            factor = sb.tile([P, HALF], F32, name="factor%d" % h)
-            nc.scalar.copy(factor[:], factors[h][:].rearrange("p c s -> p (c s)"))
             nc.vector.tensor_tensor(
-                window[:].indirect(scatter_list[:, 16 * h : 16 * (h + 1)]), shares[h][:], factor[:], ALU.mult
+                window[:].indirect(scatter_list[:, 16 * h : 16 * (h + 1)]), shares[h][:], factors[h][:], ALU.mult
             )
 
         start = 0

@@ -24,8 +24,7 @@ CHUNK = 128
 CHUNKS = I // CHUNK
 HALF = I // 2
 LIVE = P - 1
-HIGH_SPLIT = 512
-STORE_WIDTHS = (512, 512, 512, 512)
+STORE_WIDTHS = (256, 512, 512, 512, 256)
 
 
 def tile_attend_interval_balanced_counts_kernel(
@@ -40,7 +39,7 @@ def tile_attend_interval_balanced_counts_kernel(
         scatter_list = sb.tile([P, I // 16], U16, name="scatter_list")
         key_words = sb.tile([P, T], U32, name="key_words")
         key_scales = sb.tile([P, T], U8, name="key_scales")
-        low_pool = sb.tile([P, T], F32, name="low_pool", tag="low_pool_then_words", align_bytes=64)
+        low_pool = sb.tile([P, T], F32, name="low_pool")
         high_pool = sb.tile([P, T], F32, name="high_pool", tag="high_pool_then_low_cols")
         q_raw = sb.tile([P, PACK, Q], F32, name="q_raw", tag="q_raw_then_old")
         lam_col = sb.tile([P, 1], F32, name="lam_col")
@@ -54,8 +53,7 @@ def tile_attend_interval_balanced_counts_kernel(
         nc.sync.dma_start(low_pool[LIVE:P, :], lowend[0:1, :])
         nc.sync.dma_start(high_pool[LIVE:P, :], highend[0:1, :])
         for r in range(4):
-            queue = nc.gpsimd if r == 3 else nc.sync
-            queue.dma_start(scale_words[32 * r : 32 * r + 4, :], keys_scales[0, 4 * r : 4 * r + 4, :].bitcast(I32))
+            nc.sync.dma_start(scale_words[32 * r : 32 * r + 4, :], keys_scales[0, 4 * r : 4 * r + 4, :].bitcast(I32))
         nc.sync.dma_start(q_raw[:], query.rearrange("(p j) q -> p j q", j=PACK))
         nc.sync.dma_start(key_words[:].bitcast(I32), keys_words[0].rearrange("p n t -> p (n t)").bitcast(I32))
         tiny = sb.tile([P, 1], F32, name="tiny")
@@ -63,21 +61,18 @@ def tile_attend_interval_balanced_counts_kernel(
         nc.sync.dma_start(lam_col[:], lam)
         nc.sync.dma_start(scatter_list[:], offs2)
         nc.sync.dma_start(fade_col[:], fade)
-        nc.vector.memset(low_pool[0:LIVE, 0 : T // 2 - 1], 0.0)
-        nc.vector.memset(low_pool[0:LIVE, T // 2 - 1 : T], 0.0)
-        nc.vector.memset(high_pool[0:LIVE, 0 : HIGH_SPLIT // 2 - 1], 0.0)
-        nc.vector.memset(high_pool[0:LIVE, HIGH_SPLIT // 2 - 1 : HIGH_SPLIT], 0.0)
+        nc.vector.memset(low_pool[0:LIVE, :].bitcast(I32), 0)
+        nc.vector.memset(high_pool[0:LIVE, :].bitcast(I32), 0)
         ident = sb.tile([P, P], F32, name="ident")
         make_identity(nc, ident[:])
-        nc.gpsimd.memset(high_pool[0:LIVE, HIGH_SPLIT:T], 0.0)
 
         q_grouped = sb.tile([P, Q, PACK], BF16, name="q_grouped", align_bytes=64)
-        nc.scalar.copy(out=q_grouped[:], in_=q_raw[:].rearrange("p j q -> p q j"))
+        nc.vector.tensor_copy(out=q_grouped[:], in_=q_raw[:].rearrange("p j q -> p q j"))
         q_codes = sb.tile([P, Q], U32, name="q_codes", tag="q_codes_then_window", align_bytes=64)
         q_scales = sb.tile([P, Q], U8, name="q_scales", align_bytes=64)
 
         low_picked = sb.tile([P, I], F32, name="low_picked")
-        nc.vector.tensor_copy(low_picked[:], low_pool[:].indirect(gather_list[:]))
+        nc.scalar.activation(low_picked[:], low_pool[:].indirect(gather_list[:]), ACT.Copy)
         high_picked = sb.tile([P, I], F32, name="high_picked")
         nc.scalar.activation(high_picked[:], high_pool[:].indirect(gather_list[:]), ACT.Copy)
         nc.vector.quantize_mx(
@@ -91,18 +86,18 @@ def tile_attend_interval_balanced_counts_kernel(
             turned.append(bank)
         low_cols = sb.tile([P, CHUNKS], F32, name="low_cols", tag="high_pool_then_low_cols")
         nc.scalar.copy(low_cols[:], turned[0][:, :, LIVE])
-        high_cols = sb.tile([P, CHUNKS], F32, name="high_cols", tag="q_raw_then_old")
+        high_cols = sb.tile([P, CHUNKS], F32, name="high_cols")
         nc.scalar.copy(high_cols[:], turned[1][:, :, LIVE])
 
         picked_scales = sb.tile([P, I], U8, name="picked_scales", align_bytes=64)
         nc.vector.tensor_copy(picked_scales[:], key_scales[:].indirect(gather_list[:]))
 
-        picked_words = sb.tile([P, I], U32, name="picked_words", tag="low_pool_then_words", align_bytes=64)
+        picked_words = sb.tile([P, I], U32, name="picked_words", align_bytes=64)
         products = []
         for c in range(CHUNKS):
             slots = slice(c * CHUNK, (c + 1) * CHUNK)
             nc.vector.tensor_copy(picked_words[:, slots], key_words[:].indirect(gather_list[:, 8 * c : 8 * (c + 1)]))
-            product = ps.tile([P, Q], F32, name="product%d" % c, tag=("low_bank", "high_bank", "bank2", "bank3")[c])
+            product = ps.tile([P, Q], F32, name="product%d" % c, tag=("low_bank", "bank1", "bank2", "bank3")[c])
             nc.tensor.matmul_mx(
                 out=product[:],
                 lhsT=picked_words[:, slots].bitcast(FP8X4),
@@ -153,37 +148,42 @@ def tile_attend_interval_balanced_counts_kernel(
         nc.vector.reciprocal(row_inv[:], row_sum[:])
 
         shares = [sb.tile([P, HALF], F32, name="share%d" % h, align_bytes=64) for h in range(2)]
-        for h in range(2):
-            nc.vector.tensor_scalar(shares[h][:], p_exp[:, h * HALF : (h + 1) * HALF], row_inv[:], None, ALU.mult)
-        share_blocks = sb.tile([P, HALF], F32, name="share_blocks", align_bytes=64)
-        nc.vector.transpose(share_blocks[:], shares[0][:])
-        share_bank = ps.tile([P, HALF], F32, name="share_bank")
-        for c in range(2):
-            cols = slice(c * CHUNK, (c + 1) * CHUNK)
-            nc.tensor.transpose(share_bank[:, cols], shares[1][:, cols], ident[:])
+        factors = [sb.tile([P, HALF], F32, name="factor%d" % h, align_bytes=64) for h in range(2)]
+        chunk_cols = [slice(c * CHUNK, (c + 1) * CHUNK) for c in range(2)]
 
-        turned_factors = []
-        for h, turned_share in enumerate((share_blocks, share_bank)):
-            group_sum = sb.tile([P, HALF // GROUP], F32, name="group_sum%d" % h)
+        def inverse_roots(turned_share, name):
+            group_sum = sb.tile([P, K], F32, name="group_sum" + name)
             nc.vector.tensor_reduce(
-                group_sum[:], turned_share[:].rearrange("p (g j) -> p g j", j=GROUP), mybir.AxisListType.X, ALU.add
+                group_sum[:], turned_share.rearrange("p (g j) -> p g j", j=GROUP), mybir.AxisListType.X, ALU.add
             )
-            turned_factor = sb.tile([P, HALF], F32, name="turned_factor%d" % h, align_bytes=64)
+            turned_factor = sb.tile([P, CHUNK], F32, name="turned_factor" + name, align_bytes=64)
             nc.scalar.activation(
                 turned_factor[:].rearrange("p (g j) -> p g j", j=GROUP),
-                group_sum[:].unsqueeze(2).to_broadcast([P, HALF // GROUP, GROUP]),
+                group_sum[:].unsqueeze(2).to_broadcast([P, K, GROUP]),
                 ACT.Abs_reciprocal_sqrt,
                 bias=tiny[:],
                 scale=1.0 / (128.0 * 128.0),
             )
-            turned_factors.append(turned_factor)
+            return turned_factor
 
-        factors = [sb.tile([P, HALF], F32, name="factor%d" % h, align_bytes=64) for h in range(2)]
-        nc.vector.transpose(factors[0][:], turned_factors[0][:])
+        for cols in chunk_cols:
+            nc.vector.tensor_scalar(shares[0][:, cols], p_exp[:, cols], row_inv[:], None, ALU.mult)
+        share_blocks = sb.tile([P, HALF], F32, name="share_blocks", align_bytes=64)
+        for cols in chunk_cols:
+            nc.vector.transpose(share_blocks[:, cols], shares[0][:, cols])
+        nc.vector.tensor_scalar(shares[1][:], p_exp[:, HALF:], row_inv[:], None, ALU.mult)
+        first_factors = [inverse_roots(share_blocks[:, chunk_cols[c]], "a%d" % c) for c in range(2)]
+
+        share_bank = ps.tile([P, HALF], F32, name="share_bank", tag="high_bank")
+        for cols in chunk_cols:
+            nc.tensor.transpose(share_bank[:, cols], shares[1][:, cols], ident[:])
+        second_factors = [inverse_roots(share_bank[:, chunk_cols[c]], "b%d" % c) for c in range(2)]
+
+        for c in range(2):
+            nc.vector.transpose(factors[0][:, chunk_cols[c]], first_factors[c][:])
         factor_bank = ps.tile([P, HALF], F32, name="factor_bank")
         for c in range(2):
-            cols = slice(c * CHUNK, (c + 1) * CHUNK)
-            nc.tensor.transpose(factor_bank[:, cols], turned_factors[1][:, cols], ident[:])
+            nc.tensor.transpose(factor_bank[:, chunk_cols[c]], second_factors[c][:], ident[:])
         nc.scalar.copy(factors[1][:], factor_bank[:])
 
         for h in range(2):

from contextlib import ExitStack

import concourse.mybir as mybir
from concourse.masks import make_identity

D, T, I, Q, K, M = 512, 2048, 512, 128, 16, 2048
FLOPS = 2 * D * Q * I
BYTES = 4 * D * Q + D * T + (D // 32) * T + 2 * 4 * T + 2 * 4 * Q + 2 * 4 * Q * M + 2 * 2 * 128 * (I // 16)

F32 = mybir.dt.float32
BF16 = mybir.dt.bfloat16
I32 = mybir.dt.int32
U32 = mybir.dt.uint32
U16 = mybir.dt.uint16
U8 = mybir.dt.uint8
FP8X4 = mybir.dt.float8_e4m3fn_x4
ALU = mybir.AluOpType
ACT = mybir.ActivationFunctionType

P = 128
PACK = 4
GROUP = Q // K
CHUNK = 128
CHUNKS = I // CHUNK
HALF = I // 2
LIVE = P - 1
STORE_WIDTHS = (256, 512, 512, 512, 256)


def tile_attend_interval_balanced_counts_kernel(
    tc, query, keys_words, keys_scales, lowend, highend, lam, old, fade, offs, offs2, out
):
    nc = tc.nc
    with ExitStack() as ctx:
        sb = ctx.enter_context(tc.tile_pool(name="sb", bufs=1))
        ps = ctx.enter_context(tc.psum_pool(name="ps", bufs=1))

        gather_list = sb.tile([P, I // 16], U16, name="gather_list")
        scatter_list = sb.tile([P, I // 16], U16, name="scatter_list")
        key_words = sb.tile([P, T], U32, name="key_words")
        key_scales = sb.tile([P, T], U8, name="key_scales")
        low_pool = sb.tile([P, T], F32, name="low_pool")
        high_pool = sb.tile([P, T], F32, name="high_pool", tag="high_pool_then_low_cols")
        q_raw = sb.tile([P, PACK, Q], F32, name="q_raw", tag="q_raw_then_old")
        lam_col = sb.tile([P, 1], F32, name="lam_col")
        fade_col = sb.tile([P, 1], F32, name="fade_col")

        scale_words = key_scales[:].bitcast(I32)
        nc.gpsimd.memset(scale_words, 0)
        one = sb.tile([P, 1], F32, name="one")
        nc.gpsimd.memset(one[:], 1.0)
        nc.sync.dma_start(gather_list[:], offs)
        nc.sync.dma_start(low_pool[LIVE:P, :], lowend[0:1, :])
        nc.sync.dma_start(high_pool[LIVE:P, :], highend[0:1, :])
        for r in range(4):
            nc.sync.dma_start(scale_words[32 * r : 32 * r + 4, :], keys_scales[0, 4 * r : 4 * r + 4, :].bitcast(I32))
        nc.sync.dma_start(q_raw[:], query.rearrange("(p j) q -> p j q", j=PACK))
        nc.sync.dma_start(key_words[:].bitcast(I32), keys_words[0].rearrange("p n t -> p (n t)").bitcast(I32))
        tiny = sb.tile([P, 1], F32, name="tiny")
        nc.scalar.activation(tiny[:], one[:], ACT.Copy, scale=1e-30)
        nc.sync.dma_start(lam_col[:], lam)
        nc.sync.dma_start(scatter_list[:], offs2)
        nc.sync.dma_start(fade_col[:], fade)
        nc.vector.memset(low_pool[0:LIVE, :].bitcast(I32), 0)
        nc.vector.memset(high_pool[0:LIVE, :].bitcast(I32), 0)
        ident = sb.tile([P, P], F32, name="ident")
        make_identity(nc, ident[:])

        q_grouped = sb.tile([P, Q, PACK], BF16, name="q_grouped", align_bytes=64)
        nc.vector.tensor_copy(out=q_grouped[:], in_=q_raw[:].rearrange("p j q -> p q j"))
        q_codes = sb.tile([P, Q], U32, name="q_codes", tag="q_codes_then_window", align_bytes=64)
        q_scales = sb.tile([P, Q], U8, name="q_scales", align_bytes=64)

        low_picked = sb.tile([P, I], F32, name="low_picked")
        nc.scalar.activation(low_picked[:], low_pool[:].indirect(gather_list[:]), ACT.Copy)
        high_picked = sb.tile([P, I], F32, name="high_picked")
        nc.scalar.activation(high_picked[:], high_pool[:].indirect(gather_list[:]), ACT.Copy)
        nc.vector.quantize_mx(
            out=q_codes[:].bitcast(FP8X4), scales=q_scales[:], in_=q_grouped[:].rearrange("p q j -> p (q j)")
        )
        turned = []
        for name, picked in (("low", low_picked), ("high", high_picked)):
            bank = ps.tile([P, CHUNKS, P], F32, name=name + "_turned", tag=name + "_bank")
            for c in range(CHUNKS):
                nc.tensor.transpose(bank[:, c, :], picked[:, c * CHUNK : (c + 1) * CHUNK], ident[:])
            turned.append(bank)
        low_cols = sb.tile([P, CHUNKS], F32, name="low_cols", tag="high_pool_then_low_cols")
        nc.scalar.copy(low_cols[:], turned[0][:, :, LIVE])
        high_cols = sb.tile([P, CHUNKS], F32, name="high_cols")
        nc.scalar.copy(high_cols[:], turned[1][:, :, LIVE])

        picked_scales = sb.tile([P, I], U8, name="picked_scales", align_bytes=64)
        nc.vector.tensor_copy(picked_scales[:], key_scales[:].indirect(gather_list[:]))

        picked_words = sb.tile([P, I], U32, name="picked_words", align_bytes=64)
        products = []
        for c in range(CHUNKS):
            slots = slice(c * CHUNK, (c + 1) * CHUNK)
            nc.vector.tensor_copy(picked_words[:, slots], key_words[:].indirect(gather_list[:, 8 * c : 8 * (c + 1)]))
            product = ps.tile([P, Q], F32, name="product%d" % c, tag=("low_bank", "bank1", "bank2", "bank3")[c])
            nc.tensor.matmul_mx(
                out=product[:],
                lhsT=picked_words[:, slots].bitcast(FP8X4),
                lhsT_scale=picked_scales[:, slots],
                rhs=q_codes[:].bitcast(FP8X4),
                rhs_scale=q_scales[:],
                start=True,
                stop=True,
            )
            products.append(product)

        window = sb.tile([P, M], F32, name="window", tag="q_codes_then_window", align_bytes=64)
        nc.gpsimd.memset(window[:], 0.0)

        early = (CHUNKS - 1) * CHUNK
        spans = (slice(0, early), slice(early, I))
        neg_margin_t = [ps.tile([P, I], F32, name="neg_margin_t%d" % h) for h in range(2)]
        for c in range(CHUNKS):
            below = sb.tile([P, Q], F32, name="below%d" % c)
            nc.scalar.activation(below[:], products[c][:], ACT.Identity, bias=low_cols[:, c : c + 1], scale=-1.0)
            neg_margin = sb.tile([P, Q], F32, name="neg_margin%d" % c)
            nc.vector.scalar_tensor_tensor(
                neg_margin[:], products[c][:], high_cols[:, c : c + 1], below[:], ALU.subtract, ALU.max
            )
            bank = neg_margin_t[c // (CHUNKS - 1)]
            nc.tensor.transpose(bank[:, c * CHUNK : (c + 1) * CHUNK], neg_margin[:], ident[:])

        old_sb = sb.tile([P, M], F32, name="old_sb", tag="q_raw_then_old")
        nc.sync.dma_start(old_sb[:], old)

        neg_score = sb.tile([P, I], F32, name="neg_score")
        neg_max = [sb.tile([P, 1], F32, name="neg_max%d" % h) for h in range(2)]
        for h in range(2):
            nc.vector.tensor_scalar(
                neg_score[:, spans[h]],
                neg_margin_t[h][:, spans[h]],
                lam_col[:],
                neg_max[0][:] if h else None,
                ALU.mult,
                ALU.min,
                accum_out=neg_max[h][:],
            )

        p_exp = sb.tile([P, I], F32, name="p_exp")
        row_sum = sb.tile([P, 1], F32, name="row_sum")
        nc.scalar.activation(p_exp[:], neg_score[:], ACT.Exp, bias=neg_max[1][:], scale=-1.0, accum_out=row_sum[:])
        row_inv = sb.tile([P, 1], F32, name="row_inv")
        nc.vector.reciprocal(row_inv[:], row_sum[:])

        shares = [sb.tile([P, HALF], F32, name="share%d" % h, align_bytes=64) for h in range(2)]
        factors = [sb.tile([P, HALF], F32, name="factor%d" % h, align_bytes=64) for h in range(2)]
        chunk_cols = [slice(c * CHUNK, (c + 1) * CHUNK) for c in range(2)]

        def inverse_roots(turned_share, name):
            group_sum = sb.tile([P, K], F32, name="group_sum" + name)
            nc.vector.tensor_reduce(
                group_sum[:], turned_share.rearrange("p (g j) -> p g j", j=GROUP), mybir.AxisListType.X, ALU.add
            )
            turned_factor = sb.tile([P, CHUNK], F32, name="turned_factor" + name, align_bytes=64)
            nc.scalar.activation(
                turned_factor[:].rearrange("p (g j) -> p g j", j=GROUP),
                group_sum[:].unsqueeze(2).to_broadcast([P, K, GROUP]),
                ACT.Abs_reciprocal_sqrt,
                bias=tiny[:],
                scale=1.0 / (128.0 * 128.0),
            )
            return turned_factor

        for cols in chunk_cols:
            nc.vector.tensor_scalar(shares[0][:, cols], p_exp[:, cols], row_inv[:], None, ALU.mult)
        share_blocks = sb.tile([P, HALF], F32, name="share_blocks", align_bytes=64)
        for cols in chunk_cols:
            nc.vector.transpose(share_blocks[:, cols], shares[0][:, cols])
        nc.vector.tensor_scalar(shares[1][:], p_exp[:, HALF:], row_inv[:], None, ALU.mult)
        first_factors = [inverse_roots(share_blocks[:, chunk_cols[c]], "a%d" % c) for c in range(2)]

        share_bank = ps.tile([P, HALF], F32, name="share_bank", tag="high_bank")
        for cols in chunk_cols:
            nc.tensor.transpose(share_bank[:, cols], shares[1][:, cols], ident[:])
        second_factors = [inverse_roots(share_bank[:, chunk_cols[c]], "b%d" % c) for c in range(2)]

        for c in range(2):
            nc.vector.transpose(factors[0][:, chunk_cols[c]], first_factors[c][:])
        factor_bank = ps.tile([P, HALF], F32, name="factor_bank")
        for c in range(2):
            nc.tensor.transpose(factor_bank[:, chunk_cols[c]], second_factors[c][:], ident[:])
        nc.scalar.copy(factors[1][:], factor_bank[:])

        for h in range(2):
            nc.vector.tensor_tensor(
                window[:].indirect(scatter_list[:, 16 * h : 16 * (h + 1)]), shares[h][:], factors[h][:], ALU.mult
            )

        start = 0
        for n, width in enumerate(STORE_WIDTHS):
            cols = slice(start, start + width)
            result = sb.tile([P, width], F32, name="result%d" % n)
            nc.vector.scalar_tensor_tensor(result[:], old_sb[:, cols], fade_col[:], window[:, cols], ALU.mult, ALU.add)
            (nc.sync, nc.scalar)[n % 2].dma_start(out[:, cols], result[:])
            start += width
